import numpy as np
import ml_dtypes


def mxq(x, axis, fmt="e4m3"):
    dtype, down = {"e4m3": (ml_dtypes.float8_e4m3fn, 7), "e5m2": (ml_dtypes.float8_e5m2, 14)}[fmt]
    v = np.moveaxis(np.asarray(x, np.float32).astype(ml_dtypes.bfloat16).astype(np.float64), axis, -1)
    blocks = v.reshape(v.shape[:-1] + (-1, 32))
    amax = np.abs(blocks).max(-1, keepdims=True)
    byte = np.maximum(np.where(amax > 0, np.frexp(amax)[1] - 1 + 127, 0) - down, 1)
    scale = np.exp2(byte - 127.0)
    codes = (blocks / scale).astype(np.float32).astype(dtype).astype(np.float64)
    return np.moveaxis((codes * scale).reshape(v.shape), -1, axis)


WIDE = False


def mx_kscale(k):
    if not WIDE:
        return np.ones(k)
    levels = np.array([10, -10, 5, -5, 0])
    if k % 512:
        return np.exp2(np.random.permutation(np.resize(levels, k // 32))).repeat(32)
    a = np.empty((k // 512, 16))
    for p in range(k // 512):
        a[p, :8] = np.random.permutation(np.resize(levels, 8))
        for g in range(8):
            far = levels[np.abs(levels - a[p, g]) >= 10]
            a[p, g + 8] = far[np.random.randint(len(far))]
    return np.exp2(a.ravel()).repeat(32)


def f64(x):
    return np.asarray(x).astype(np.float64)


def striped8(idx):
    return np.asarray(idx).reshape(8, -1, 16).transpose(0, 2, 1).reshape(128, -1).astype(np.uint16)


def unstriped8(offs):
    return offs.reshape(8, 16, -1).transpose(0, 2, 1).reshape(8, -1).astype(np.int64)


def pick8(x, idx, run):
    r = np.arange(len(x))
    return x[r[:, None], idx[r % (8 * run) // run]]


E2M1 = np.array([0.0, 0.5, 1.0, 1.5, 2.0, 3.0, 4.0, 6.0, -0.0, -0.5, -1.0, -1.5, -2.0, -3.0, -4.0, -6.0])


def pack_weight(w, fmt):
    k, n = w.shape
    w = f64(np.asarray(w, np.float32).astype(ml_dtypes.bfloat16)).reshape(k // 32, 32, n)
    amax = np.abs(w).max(1)
    if fmt == "e4m3":
        byte = np.frexp(amax)[1] - 1 + 127 - 7
    else:
        mant, ex = np.frexp(amax / 6.0)
        byte = np.where(mant > 0.5, ex, ex - 1) + 127
    byte = np.clip(np.where(amax > 0, byte, 1), 1, 254)
    scaled = (w * np.exp2(127.0 - byte)[:, None, :]).reshape(k, n).astype(np.float32)
    by_word = np.ascontiguousarray(scaled.reshape(k // 512, 128, 4, n).transpose(0, 1, 3, 2))
    if fmt == "e4m3":
        words = by_word.astype(ml_dtypes.float8_e4m3fn).view(np.uint8)
    else:
        c = by_word.astype(ml_dtypes.float4_e2m1fn).view(np.uint8) & 0xF
        words = (c[..., 0::2] | (c[..., 1::2] << 4)).reshape(k // 512, 128, 2 * n)
    return np.ascontiguousarray(words), np.ascontiguousarray(byte.astype(np.uint8).reshape(k // 512, 16, n))


def unpack_weight(words, scales, fmt):
    g, _, n = scales.shape
    words = np.ascontiguousarray(words).reshape(g, 128, n, -1)
    if fmt == "e4m3":
        vals = words.view(ml_dtypes.float8_e4m3fn).astype(np.float64)
    else:
        nib = np.empty((g, 128, n, 4), np.uint8)
        nib[..., 0::2] = words & 0xF
        nib[..., 1::2] = words >> 4
        vals = E2M1[nib]
    vals = vals * np.repeat(np.exp2(scales.astype(np.float64) - 127.0), 8, axis=1)[..., None]
    return vals.transpose(0, 1, 3, 2).reshape(g * 512, n)


D, T, I, Q = 512, 1024, 512, 128


def setup_inputs():
    n = np.random.standard_normal
    idx = np.stack([np.random.permutation(T)[:I] for _ in range(8)])
    idx2 = np.stack([np.random.permutation(T)[:I] for _ in range(8)])
    fd = mx_kscale(D)
    keysp = pack_weight(n((D, T)) / fd[:, None], "e4m3")
    return {
        "query": (n((D, Q)) * 0.9 / np.sqrt(D) * fd[:, None]).astype(np.float32),
        "query2": (n((D, Q)) * 0.9 / np.sqrt(D) * fd[:, None]).astype(np.float32),
        "keys_words": keysp[0],
        "keys_scales": keysp[1],
        "lam": (np.random.uniform(0.5, 1.3, (Q, 1))).astype(np.float32),
        "width": (np.random.uniform(0.3, 0.8, (Q, 1))).astype(np.float32),
        "old": (np.random.uniform(0.0, 2.0, (Q, T))).astype(np.float32),
        "fade": (np.random.uniform(0.3, 0.9, (Q, 1))).astype(np.float32),
        "offs": striped8(idx),
        "offs2": striped8(idx2),
    }


def reference(query, query2, keys_words, keys_scales, lam, width, old, fade, offs, offs2):
    idx = unstriped8(offs)
    idx2 = unstriped8(offs2)
    keysu = unpack_weight(keys_words, keys_scales, "e4m3")
    queryq = mxq(f64(query), 0, "e4m3")
    a = queryq.T @ keysu
    query2q = mxq(f64(query2), 0, "e4m3")
    b = query2q.T @ keysu
    s = (np.maximum(pick8(a, idx, 16), pick8(b, idx2, 16)) - np.maximum(pick8(a, idx2, 16), pick8(b, idx, 16))) * f64(lam)
    ce = (s - np.mean(s, axis=1, keepdims=True)) / f64(width)
    p = 1.0 / (np.square(ce) + 1.0)
    w = p / np.sum(p, axis=1, keepdims=True)
    ws = w * 512.0
    wf = np.zeros((Q, T))
    wf[np.arange(Q)[:, None], idx[np.arange(Q) % 128 // 16]] = ws
    y = f64(old) * f64(fade) + wf
    return y

@@ -1,0 +1,153 @@
+from contextlib import ExitStack
+
+import concourse.mybir as mybir
+
+D, T, I, Q = 512, 1024, 512, 128
+FLOPS = 2 * 2 * D * T * Q
+
+F32 = mybir.dt.float32
+BF16 = mybir.dt.bfloat16
+I32 = mybir.dt.int32
+U32 = mybir.dt.uint32
+U16 = mybir.dt.uint16
+U8 = mybir.dt.uint8
+FP8X4 = mybir.dt.float8_e4m3fn_x4
+ALU = mybir.AluOpType
+ACT = mybir.ActivationFunctionType
+
+P = 128
+PACK = 4
+PIECE = 256
+PIECES = T // PIECE
+HALF = I // 2
+LIST_COLS = 16
+
+
+def tile_attend_exchanged_typical_counts_heads_kernel(
+    tc, query, query2, keys_words, keys_scales, lam, width, old, fade, offs, offs2, out
+):
+    nc = tc.nc
+    with ExitStack() as ctx:
+        sb = ctx.enter_context(tc.tile_pool(name="sb", bufs=1))
+        psum = ctx.enter_context(tc.psum_pool(name="psum", bufs=1))
+
+        first_list = sb.tile([P, I // LIST_COLS], U16, name="first_list")
+        second_list = sb.tile([P, I // LIST_COLS], U16, name="second_list")
+
+        key_scales = sb.tile([P, PIECE], U8, name="key_scales", align_bytes=64)
+        nc.vector.memset(key_scales[:].bitcast(I32), 0)
+        placed = sb.tile([P, T], F32, name="placed")
+        nc.vector.memset(placed[:], 0.0)
+        unit = sb.tile([P, 1], F32, name="unit")
+        nc.vector.memset(unit[:], float(I * I))
+
+        words = keys_words[0].rearrange("p n t -> p (n t)").bitcast(I32)
+        scale_words = keys_scales[0].bitcast(I32)
+        raw = [sb.tile([P, PACK, Q], F32, name="raw%d" % n) for n in range(2)]
+        early = 2 * PIECE
+        keys = [sb.tile([P, w], I32, name="keys%d" % n, align_bytes=64) for n, w in enumerate((early, T - early))]
+        nc.sync.dma_start(raw[0][:], query.rearrange("(p j) q -> p j q", j=PACK))
+        nc.sync.dma_start(keys[0][:], words[:, 0:early])
+        for quad in range(4):
+            nc.sync.dma_start(
+                key_scales[32 * quad : 32 * quad + 16, :].bitcast(I32),
+                scale_words[4 * quad : 4 * quad + 4, :].rearrange("r (j c) -> j r c", j=PIECES),
+            )
+        nc.sync.dma_start(raw[1][:], query2.rearrange("(p j) q -> p j q", j=PACK))
+        nc.sync.dma_start(keys[1][:], words[:, early:T])
+        nc.sync.dma_start(first_list[:], offs)
+        nc.sync.dma_start(second_list[:], offs2)
+        width_col = sb.tile([P, 1], F32, name="width_col")
+        lam_col = sb.tile([P, 1], F32, name="lam_col")
+        fade_col = sb.tile([P, 1], F32, name="fade_col")
+        old_sb = sb.tile([P, T], F32, name="old_sb")
+        nc.sync.dma_start(width_col[:], width)
+        nc.sync.dma_start(lam_col[:], lam)
+        nc.sync.dma_start(fade_col[:], fade)
+        nc.sync.dma_start(old_sb[:], old)
+
+
+        scores = []
+        for n in range(2):
+            grouped = sb.tile([P, Q, PACK], BF16, name="grouped%d" % n, align_bytes=64)
+            nc.vector.tensor_copy(
+                grouped[:].rearrange("p (c i) j -> p c j i", i=4),
+                raw[n][:].rearrange("p j (c i) -> p c j i", i=4),
+            )
+            codes = sb.tile([P, Q], U32, name="codes%d" % n, align_bytes=64)
+            scales = sb.tile([P, Q], U8, name="scales%d" % n, align_bytes=64)
+            nc.vector.quantize_mx(
+                out=codes[:].bitcast(FP8X4), scales=scales[:], in_=grouped[:].rearrange("p q j -> p (q j)")
+            )
+            score = sb.tile([P, T], F32, name="score%d" % n)
+            for j in range(PIECES):
+                bank = psum.tile([P, PIECE], F32, name="bank%d_%d" % (n, j))
+                cols = slice((j % 2) * PIECE, (j % 2 + 1) * PIECE)
+                nc.tensor.matmul_mx(
+                    out=bank[:],
+                    lhsT=codes[:].bitcast(FP8X4),
+                    lhsT_scale=scales[:],
+                    rhs=keys[j // 2][:, cols].bitcast(FP8X4),
+                    rhs_scale=key_scales[4 * j : P, :],
+                    start=True,
+                    stop=True,
+                )
+                if n == 0 and j == PIECES - 1:
+                    nc.vector.tensor_copy(score[:, j * PIECE : (j + 1) * PIECE], bank[:])
+                else:
+                    nc.scalar.copy(score[:, j * PIECE : (j + 1) * PIECE], bank[:])
+            scores.append(score)
+        a, b = scores
+
+        a_first = sb.tile([P, I], F32, name="a_first")
+        a_second = sb.tile([P, I], F32, name="a_second")
+        b_first = sb.tile([P, I], F32, name="b_first")
+        b_second = sb.tile([P, I], F32, name="b_second")
+        nc.vector.tensor_copy(a_first[:], a[:].indirect(first_list[:]))
+        nc.vector.tensor_copy(a_second[:], a[:].indirect(second_list[:]))
+        straight = sb.tile([P, I], F32, name="straight")
+        crossed = sb.tile([P, I], F32, name="crossed")
+        for h in range(2):
+            slots = slice(h * HALF, (h + 1) * HALF)
+            entries = slice(h * HALF // LIST_COLS, (h + 1) * HALF // LIST_COLS)
+            nc.scalar.activation(b_second[:, slots], b[:].indirect(second_list[:, entries]), ACT.Copy)
+            nc.scalar.activation(b_first[:, slots], b[:].indirect(first_list[:, entries]), ACT.Copy)
+            nc.vector.tensor_tensor(straight[:, slots], a_first[:, slots], b_second[:, slots], ALU.max)
+            nc.vector.tensor_tensor(crossed[:, slots], a_second[:, slots], b_first[:, slots], ALU.max)
+
+        inv_width = sb.tile([P, 1], F32, name="inv_width", tag="score1")
+        nc.scalar.activation(inv_width[:], width_col[:], ACT.Abs_reciprocal_sqrt, scale=width_col[:])
+        gain = sb.tile([P, 1], F32, name="gain")
+        nc.scalar.activation(gain[:], inv_width[:], ACT.Square, scale=lam_col[:])
+
+        diff = sb.tile([P, I], F32, name="diff")
+        diff_sum = sb.tile([P, 1], F32, name="diff_sum")
+        nc.vector.scalar_tensor_tensor(
+            diff[:], straight[:], 1.0, crossed[:], ALU.mult, ALU.subtract, accum_out=diff_sum[:]
+        )
+        spread = sb.tile([P, I], F32, name="spread")
+        root = sb.tile([P, I], F32, name="root")
+        part = sb.tile([P, I], F32, name="part")
+        part_sum = sb.tile([P, 1], F32, name="part_sum")
+        cut = 320
+        centred = sb.tile([P, I - cut], F32, name="centred")
+        nc.scalar.activation(spread[:, 0:cut], diff[:, 0:cut], ACT.Square, scale=-float(I), bias=diff_sum[:])
+        nc.vector.tensor_scalar(centred[:], diff[:, cut:I], float(I), diff_sum[:], ALU.mult, ALU.subtract)
+        nc.vector.tensor_tensor(spread[:, cut:I], centred[:], centred[:], ALU.mult)
+        for slots in (slice(0, cut), slice(cut, I)):
+            nc.scalar.activation(
+                root[:, slots], spread[:, slots], ACT.Abs_reciprocal_sqrt, scale=gain[:], bias=unit[:]
+            )
+        nc.scalar.activation(part[:], root[:], ACT.Square, accum_out=part_sum[:])
+        inv_sum = sb.tile([P, 1], F32, name="inv_sum")
+        nc.vector.reciprocal(inv_sum[:], part_sum[:])
+        weight = sb.tile([P, I], F32, name="weight")
+        nc.vector.tensor_scalar(weight[:], part[:], inv_sum[:], float(I), ALU.mult, ALU.mult)
+        nc.vector.tensor_copy(placed[:].indirect(first_list[:]), weight[:])
+
+        result = sb.tile([P, T], F32, name="result")
+        for j, cols in enumerate((slice(0, 256), slice(256, 576), slice(576, 896), slice(896, 1024))):
+            nc.vector.scalar_tensor_tensor(
+                result[:, cols], old_sb[:, cols], fade_col[:], placed[:, cols], ALU.mult, ALU.add
+            )
+            (nc.sync, nc.scalar)[j % 2].dma_start(out[:, cols], result[:, cols])

@@ -66,6 +66,8 @@ def tile_attend_exchanged_typical_counts_heads_kernel(
         nc.sync.dma_start(fade_col[:], fade)
         nc.sync.dma_start(old_sb[:], old)
 
+        warm = sb.tile([P, 1], F32, name="warm")
+        nc.scalar.activation(warm[:], unit[:], ACT.Abs_reciprocal_sqrt)
 
         scores = []
         for n in range(2):

@@ -53,8 +53,8 @@ def tile_attend_exchanged_typical_counts_heads_kernel(
                 key_scales[32 * quad : 32 * quad + 16, :].bitcast(I32),
                 scale_words[4 * quad : 4 * quad + 4, :].rearrange("r (j c) -> j r c", j=PIECES),
             )
-        nc.sync.dma_start(raw[1][:], query2.rearrange("(p j) q -> p j q", j=PACK))
         nc.sync.dma_start(keys[1][:], words[:, early:T])
+        nc.sync.dma_start(raw[1][:], query2.rearrange("(p j) q -> p j q", j=PACK))
         nc.sync.dma_start(first_list[:], offs)
         nc.sync.dma_start(second_list[:], offs2)
         width_col = sb.tile([P, 1], F32, name="width_col")
@@ -94,49 +94,65 @@ def tile_attend_exchanged_typical_counts_heads_kernel(
                     start=True,
                     stop=True,
                 )
-                if n == 0 and j == PIECES - 1:
+                if n == 1 and j == 1:
                     nc.vector.tensor_copy(score[:, j * PIECE : (j + 1) * PIECE], bank[:])
                 else:
                     nc.scalar.copy(score[:, j * PIECE : (j + 1) * PIECE], bank[:])
             scores.append(score)
         a, b = scores
 
-        a_first = sb.tile([P, I], F32, name="a_first")
-        a_second = sb.tile([P, I], F32, name="a_second")
-        b_first = sb.tile([P, I], F32, name="b_first")
-        b_second = sb.tile([P, I], F32, name="b_second")
-        nc.vector.tensor_copy(a_first[:], a[:].indirect(first_list[:]))
-        nc.vector.tensor_copy(a_second[:], a[:].indirect(second_list[:]))
-        straight = sb.tile([P, I], F32, name="straight")
-        crossed = sb.tile([P, I], F32, name="crossed")
-        for h in range(2):
-            slots = slice(h * HALF, (h + 1) * HALF)
-            entries = slice(h * HALF // LIST_COLS, (h + 1) * HALF // LIST_COLS)
-            nc.scalar.activation(b_second[:, slots], b[:].indirect(second_list[:, entries]), ACT.Copy)
-            nc.scalar.activation(b_first[:, slots], b[:].indirect(first_list[:, entries]), ACT.Copy)
-            nc.vector.tensor_tensor(straight[:, slots], a_first[:, slots], b_second[:, slots], ALU.max)
-            nc.vector.tensor_tensor(crossed[:, slots], a_second[:, slots], b_first[:, slots], ALU.max)
+        low, high = slice(0, HALF // LIST_COLS), slice(HALF // LIST_COLS, I // LIST_COLS)
+
+        def half(name):
+            return sb.tile([P, HALF], F32, name=name)
+
+        a_first_low, a_first_high = half("a_first_low"), half("a_first_high")
+        a_second_low = half("a_second_low")
+        a_second_high = sb.tile([P, HALF], F32, name="a_second_high", tag="keys0", align_bytes=64)
+        b_first_low, b_first_high = half("b_first_low"), half("b_first_high")
+        b_second_low, b_second_high = half("b_second_low"), half("b_second_high")
+        nc.vector.tensor_copy(a_first_low[:], a[:].indirect(first_list[:, low]))
+        nc.vector.tensor_copy(a_second_low[:], a[:].indirect(second_list[:, low]))
+        nc.vector.tensor_copy(a_second_high[:], a[:].indirect(second_list[:, high]))
+        nc.vector.tensor_copy(b_second_low[:], b[:].indirect(second_list[:, low]))
+        nc.scalar.activation(a_first_high[:], a[:].indirect(first_list[:, high]), ACT.Copy)
+        nc.scalar.activation(b_first_low[:], b[:].indirect(first_list[:, low]), ACT.Copy)
+        nc.scalar.activation(b_second_high[:], b[:].indirect(second_list[:, high]), ACT.Copy)
+        nc.scalar.activation(b_first_high[:], b[:].indirect(first_list[:, high]), ACT.Copy)
+        straight_low, straight_high = half("straight_low"), half("straight_high")
+        crossed_low, crossed_high = half("crossed_low"), half("crossed_high")
+        diff_low = half("diff_low")
+        shifted_low, shifted_high = half("shifted_low"), half("shifted_high")
+        low_sum = sb.tile([P, 1], F32, name="low_sum")
+        low_mean = sb.tile([P, 1], F32, name="low_mean")
+        rest_sum = sb.tile([P, 1], F32, name="rest_sum")
+        nc.vector.tensor_tensor(crossed_low[:], a_second_low[:], b_first_low[:], ALU.max)
+        nc.vector.tensor_tensor(straight_low[:], a_first_low[:], b_second_low[:], ALU.max)
+        nc.vector.tensor_tensor(straight_high[:], a_first_high[:], b_second_high[:], ALU.max)
+        nc.vector.scalar_tensor_tensor(
+            diff_low[:], straight_low[:], 1.0, crossed_low[:], ALU.mult, ALU.subtract, accum_out=low_sum[:]
+        )
+        nc.vector.tensor_tensor(crossed_high[:], a_second_high[:], b_first_high[:], ALU.max)
+        nc.vector.tensor_scalar(low_mean[:], low_sum[:], 1.0 / HALF, None, ALU.mult)
+        nc.vector.scalar_tensor_tensor(
+            shifted_high[:], straight_high[:], low_mean[:], crossed_high[:], ALU.subtract, ALU.subtract,
+            accum_out=rest_sum[:],
+        )
+        nc.vector.tensor_scalar(shifted_low[:], diff_low[:], low_mean[:], None, ALU.subtract)
 
         inv_width = sb.tile([P, 1], F32, name="inv_width", tag="score1")
         nc.scalar.activation(inv_width[:], width_col[:], ACT.Abs_reciprocal_sqrt, scale=width_col[:])
         gain = sb.tile([P, 1], F32, name="gain")
         nc.scalar.activation(gain[:], inv_width[:], ACT.Square, scale=lam_col[:])
 
-        diff = sb.tile([P, I], F32, name="diff")
-        diff_sum = sb.tile([P, 1], F32, name="diff_sum")
-        nc.vector.scalar_tensor_tensor(
-            diff[:], straight[:], 1.0, crossed[:], ALU.mult, ALU.subtract, accum_out=diff_sum[:]
-        )
         spread = sb.tile([P, I], F32, name="spread")
         root = sb.tile([P, I], F32, name="root")
         part = sb.tile([P, I], F32, name="part")
         part_sum = sb.tile([P, 1], F32, name="part_sum")
-        cut = 320
-        centred = sb.tile([P, I - cut], F32, name="centred")
-        nc.scalar.activation(spread[:, 0:cut], diff[:, 0:cut], ACT.Square, scale=-float(I), bias=diff_sum[:])
-        nc.vector.tensor_scalar(centred[:], diff[:, cut:I], float(I), diff_sum[:], ALU.mult, ALU.subtract)
-        nc.vector.tensor_tensor(spread[:, cut:I], centred[:], centred[:], ALU.mult)
-        for slots in (slice(0, cut), slice(cut, I)):
+        halves = ((slice(HALF, I), shifted_high), (slice(0, HALF), shifted_low))
+        for slots, shifted in halves:
+            nc.scalar.activation(spread[:, slots], shifted[:], ACT.Square, scale=-float(I), bias=rest_sum[:])
+        for slots, shifted in halves:
             nc.scalar.activation(
                 root[:, slots], spread[:, slots], ACT.Abs_reciprocal_sqrt, scale=gain[:], bias=unit[:]
             )
@@ -148,7 +164,7 @@ def tile_attend_exchanged_typical_counts_heads_kernel(
         nc.vector.tensor_copy(placed[:].indirect(first_list[:]), weight[:])
 
         result = sb.tile([P, T], F32, name="result")
-        for j, cols in enumerate((slice(0, 256), slice(256, 576), slice(576, 896), slice(896, 1024))):
+        for j, cols in enumerate((slice(0, 256), slice(256, 512), slice(512, 768), slice(768, 1024))):
             nc.vector.scalar_tensor_tensor(
                 result[:, cols], old_sb[:, cols], fade_col[:], placed[:, cols], ALU.mult, ALU.add
             )

@@ -106,31 +106,30 @@ def tile_attend_exchanged_typical_counts_heads_kernel(
         def half(name):
             return sb.tile([P, HALF], F32, name=name)
 
-        a_first_low, a_first_high = half("a_first_low"), half("a_first_high")
-        a_second_low = half("a_second_low")
-        a_second_high = sb.tile([P, HALF], F32, name="a_second_high", tag="keys0", align_bytes=64)
-        b_first_low, b_first_high = half("b_first_low"), half("b_first_high")
-        b_second_low, b_second_high = half("b_second_low"), half("b_second_high")
-        nc.vector.tensor_copy(a_first_low[:], a[:].indirect(first_list[:, low]))
-        nc.vector.tensor_copy(a_second_low[:], a[:].indirect(second_list[:, low]))
-        nc.vector.tensor_copy(a_second_high[:], a[:].indirect(second_list[:, high]))
-        nc.vector.tensor_copy(b_second_low[:], b[:].indirect(second_list[:, low]))
+        base, a_first_high = half("base"), half("a_first_high")
+        a_second_rel = sb.tile([P, HALF], F32, name="a_second_rel", tag="keys0", align_bytes=64)
+        b_first_rel, b_second_rel = half("b_first_rel"), half("b_second_rel")
+        a_second_high = sb.tile([P, HALF], F32, name="a_second_high", tag="keys1", align_bytes=64)
+        b_first_high, b_second_high = half("b_first_high"), half("b_second_high")
+        nc.vector.tensor_copy(base[:], a[:].indirect(first_list[:, low]))
+        nc.vector.tensor_tensor(a_second_rel[:], a[:].indirect(second_list[:, low]), base[:], ALU.subtract)
+        nc.vector.tensor_tensor(b_first_rel[:], b[:].indirect(first_list[:, low]), base[:], ALU.subtract)
+        nc.vector.tensor_tensor(b_second_rel[:], b[:].indirect(second_list[:, low]), base[:], ALU.subtract)
         nc.scalar.activation(a_first_high[:], a[:].indirect(first_list[:, high]), ACT.Copy)
-        nc.scalar.activation(b_first_low[:], b[:].indirect(first_list[:, low]), ACT.Copy)
         nc.scalar.activation(b_second_high[:], b[:].indirect(second_list[:, high]), ACT.Copy)
+        nc.scalar.activation(a_second_high[:], a[:].indirect(second_list[:, high]), ACT.Copy)
         nc.scalar.activation(b_first_high[:], b[:].indirect(first_list[:, high]), ACT.Copy)
-        straight_low, straight_high = half("straight_low"), half("straight_high")
+        straight_high = half("straight_high")
         crossed_low, crossed_high = half("crossed_low"), half("crossed_high")
         diff_low = half("diff_low")
         shifted_low, shifted_high = half("shifted_low"), half("shifted_high")
         low_sum = sb.tile([P, 1], F32, name="low_sum")
         low_mean = sb.tile([P, 1], F32, name="low_mean")
         rest_sum = sb.tile([P, 1], F32, name="rest_sum")
-        nc.vector.tensor_tensor(crossed_low[:], a_second_low[:], b_first_low[:], ALU.max)
-        nc.vector.tensor_tensor(straight_low[:], a_first_low[:], b_second_low[:], ALU.max)
+        nc.vector.tensor_tensor(crossed_low[:], a_second_rel[:], b_first_rel[:], ALU.max)
         nc.vector.tensor_tensor(straight_high[:], a_first_high[:], b_second_high[:], ALU.max)
         nc.vector.scalar_tensor_tensor(
-            diff_low[:], straight_low[:], 1.0, crossed_low[:], ALU.mult, ALU.subtract, accum_out=low_sum[:]
+            diff_low[:], b_second_rel[:], 0.0, crossed_low[:], ALU.max, ALU.subtract, accum_out=low_sum[:]
         )
         nc.vector.tensor_tensor(crossed_high[:], a_second_high[:], b_first_high[:], ALU.max)
         nc.vector.tensor_scalar(low_mean[:], low_sum[:], 1.0 / HALF, None, ALU.mult)

@@ -94,7 +94,7 @@ def tile_attend_exchanged_typical_counts_heads_kernel(
                     start=True,
                     stop=True,
                 )
-                if n == 1 and j == 1:
+                if n == 1 and j < 2:
                     nc.vector.tensor_copy(score[:, j * PIECE : (j + 1) * PIECE], bank[:])
                 else:
                     nc.scalar.copy(score[:, j * PIECE : (j + 1) * PIECE], bank[:])

from contextlib import ExitStack

import concourse.mybir as mybir

D, T, I, Q = 512, 1024, 512, 128
FLOPS = 2 * 2 * D * T * Q

F32 = mybir.dt.float32
BF16 = mybir.dt.bfloat16
I32 = mybir.dt.int32
U32 = mybir.dt.uint32
U16 = mybir.dt.uint16
U8 = mybir.dt.uint8
FP8X4 = mybir.dt.float8_e4m3fn_x4
ALU = mybir.AluOpType
ACT = mybir.ActivationFunctionType

P = 128
PACK = 4
PIECE = 256
PIECES = T // PIECE
HALF = I // 2
LIST_COLS = 16


def tile_attend_exchanged_typical_counts_heads_kernel(
    tc, query, query2, keys_words, keys_scales, lam, width, old, fade, offs, offs2, out
):
    nc = tc.nc
    with ExitStack() as ctx:
        sb = ctx.enter_context(tc.tile_pool(name="sb", bufs=1))
        psum = ctx.enter_context(tc.psum_pool(name="psum", bufs=1))

        first_list = sb.tile([P, I // LIST_COLS], U16, name="first_list")
        second_list = sb.tile([P, I // LIST_COLS], U16, name="second_list")

        key_scales = sb.tile([P, PIECE], U8, name="key_scales", align_bytes=64)
        nc.vector.memset(key_scales[:].bitcast(I32), 0)
        placed = sb.tile([P, T], F32, name="placed")
        nc.vector.memset(placed[:], 0.0)
        unit = sb.tile([P, 1], F32, name="unit")
        nc.vector.memset(unit[:], float(I * I))

        words = keys_words[0].rearrange("p n t -> p (n t)").bitcast(I32)
        scale_words = keys_scales[0].bitcast(I32)
        raw = [sb.tile([P, PACK, Q], F32, name="raw%d" % n) for n in range(2)]
        early = 2 * PIECE
        keys = [sb.tile([P, w], I32, name="keys%d" % n, align_bytes=64) for n, w in enumerate((early, T - early))]
        nc.sync.dma_start(raw[0][:], query.rearrange("(p j) q -> p j q", j=PACK))
        nc.sync.dma_start(keys[0][:], words[:, 0:early])
        for quad in range(4):
            nc.sync.dma_start(
                key_scales[32 * quad : 32 * quad + 16, :].bitcast(I32),
                scale_words[4 * quad : 4 * quad + 4, :].rearrange("r (j c) -> j r c", j=PIECES),
            )
        nc.sync.dma_start(keys[1][:], words[:, early:T])
        nc.sync.dma_start(raw[1][:], query2.rearrange("(p j) q -> p j q", j=PACK))
        nc.sync.dma_start(first_list[:], offs)
        nc.sync.dma_start(second_list[:], offs2)
        width_col = sb.tile([P, 1], F32, name="width_col")
        lam_col = sb.tile([P, 1], F32, name="lam_col")
        fade_col = sb.tile([P, 1], F32, name="fade_col")
        old_sb = sb.tile([P, T], F32, name="old_sb")
        nc.sync.dma_start(width_col[:], width)
        nc.sync.dma_start(lam_col[:], lam)
        nc.sync.dma_start(fade_col[:], fade)
        nc.sync.dma_start(old_sb[:], old)

        warm = sb.tile([P, 1], F32, name="warm")
        nc.scalar.activation(warm[:], unit[:], ACT.Abs_reciprocal_sqrt)

        scores = []
        for n in range(2):
            grouped = sb.tile([P, Q, PACK], BF16, name="grouped%d" % n, align_bytes=64)
            nc.vector.tensor_copy(
                grouped[:].rearrange("p (c i) j -> p c j i", i=4),
                raw[n][:].rearrange("p j (c i) -> p c j i", i=4),
            )
            codes = sb.tile([P, Q], U32, name="codes%d" % n, align_bytes=64)
            scales = sb.tile([P, Q], U8, name="scales%d" % n, align_bytes=64)
            nc.vector.quantize_mx(
                out=codes[:].bitcast(FP8X4), scales=scales[:], in_=grouped[:].rearrange("p q j -> p (q j)")
            )
            score = sb.tile([P, T], F32, name="score%d" % n)
            for j in range(PIECES):
                bank = psum.tile([P, PIECE], F32, name="bank%d_%d" % (n, j))
                cols = slice((j % 2) * PIECE, (j % 2 + 1) * PIECE)
                nc.tensor.matmul_mx(
                    out=bank[:],
                    lhsT=codes[:].bitcast(FP8X4),
                    lhsT_scale=scales[:],
                    rhs=keys[j // 2][:, cols].bitcast(FP8X4),
                    rhs_scale=key_scales[4 * j : P, :],
                    start=True,
                    stop=True,
                )
                if n == 1 and j < 2:
                    nc.vector.tensor_copy(score[:, j * PIECE : (j + 1) * PIECE], bank[:])
                else:
                    nc.scalar.copy(score[:, j * PIECE : (j + 1) * PIECE], bank[:])
            scores.append(score)
        a, b = scores

        low, high = slice(0, HALF // LIST_COLS), slice(HALF // LIST_COLS, I // LIST_COLS)

        def half(name):
            return sb.tile([P, HALF], F32, name=name)

        base, a_first_high = half("base"), half("a_first_high")
        a_second_rel = sb.tile([P, HALF], F32, name="a_second_rel", tag="keys0", align_bytes=64)
        b_first_rel, b_second_rel = half("b_first_rel"), half("b_second_rel")
        a_second_high = sb.tile([P, HALF], F32, name="a_second_high", tag="keys1", align_bytes=64)
        b_first_high, b_second_high = half("b_first_high"), half("b_second_high")
        nc.vector.tensor_copy(base[:], a[:].indirect(first_list[:, low]))
        nc.vector.tensor_tensor(a_second_rel[:], a[:].indirect(second_list[:, low]), base[:], ALU.subtract)
        nc.vector.tensor_tensor(b_first_rel[:], b[:].indirect(first_list[:, low]), base[:], ALU.subtract)
        nc.vector.tensor_tensor(b_second_rel[:], b[:].indirect(second_list[:, low]), base[:], ALU.subtract)
        nc.scalar.activation(a_first_high[:], a[:].indirect(first_list[:, high]), ACT.Copy)
        nc.scalar.activation(b_second_high[:], b[:].indirect(second_list[:, high]), ACT.Copy)
        nc.scalar.activation(a_second_high[:], a[:].indirect(second_list[:, high]), ACT.Copy)
        nc.scalar.activation(b_first_high[:], b[:].indirect(first_list[:, high]), ACT.Copy)
        straight_high = half("straight_high")
        crossed_low, crossed_high = half("crossed_low"), half("crossed_high")
        diff_low = half("diff_low")
        shifted_low, shifted_high = half("shifted_low"), half("shifted_high")
        low_sum = sb.tile([P, 1], F32, name="low_sum")
        low_mean = sb.tile([P, 1], F32, name="low_mean")
        rest_sum = sb.tile([P, 1], F32, name="rest_sum")
        nc.vector.tensor_tensor(crossed_low[:], a_second_rel[:], b_first_rel[:], ALU.max)
        nc.vector.tensor_tensor(straight_high[:], a_first_high[:], b_second_high[:], ALU.max)
        nc.vector.scalar_tensor_tensor(
            diff_low[:], b_second_rel[:], 0.0, crossed_low[:], ALU.max, ALU.subtract, accum_out=low_sum[:]
        )
        nc.vector.tensor_tensor(crossed_high[:], a_second_high[:], b_first_high[:], ALU.max)
        nc.vector.tensor_scalar(low_mean[:], low_sum[:], 1.0 / HALF, None, ALU.mult)
        nc.vector.scalar_tensor_tensor(
            shifted_high[:], straight_high[:], low_mean[:], crossed_high[:], ALU.subtract, ALU.subtract,
            accum_out=rest_sum[:],
        )
        nc.vector.tensor_scalar(shifted_low[:], diff_low[:], low_mean[:], None, ALU.subtract)

        inv_width = sb.tile([P, 1], F32, name="inv_width", tag="score1")
        nc.scalar.activation(inv_width[:], width_col[:], ACT.Abs_reciprocal_sqrt, scale=width_col[:])
        gain = sb.tile([P, 1], F32, name="gain")
        nc.scalar.activation(gain[:], inv_width[:], ACT.Square, scale=lam_col[:])

        spread = sb.tile([P, I], F32, name="spread")
        root = sb.tile([P, I], F32, name="root")
        part = sb.tile([P, I], F32, name="part")
        part_sum = sb.tile([P, 1], F32, name="part_sum")
        halves = ((slice(HALF, I), shifted_high), (slice(0, HALF), shifted_low))
        for slots, shifted in halves:
            nc.scalar.activation(spread[:, slots], shifted[:], ACT.Square, scale=-float(I), bias=rest_sum[:])
        for slots, shifted in halves:
            nc.scalar.activation(
                root[:, slots], spread[:, slots], ACT.Abs_reciprocal_sqrt, scale=gain[:], bias=unit[:]
            )
        nc.scalar.activation(part[:], root[:], ACT.Square, accum_out=part_sum[:])
        inv_sum = sb.tile([P, 1], F32, name="inv_sum")
        nc.vector.reciprocal(inv_sum[:], part_sum[:])
        weight = sb.tile([P, I], F32, name="weight")
        nc.vector.tensor_scalar(weight[:], part[:], inv_sum[:], float(I), ALU.mult, ALU.mult)
        nc.vector.tensor_copy(placed[:].indirect(first_list[:]), weight[:])

        result = sb.tile([P, T], F32, name="result")
        for j, cols in enumerate((slice(0, 256), slice(256, 512), slice(512, 768), slice(768, 1024))):
            nc.vector.scalar_tensor_tensor(
                result[:, cols], old_sb[:, cols], fade_col[:], placed[:, cols], ALU.mult, ALU.add
            )
            (nc.sync, nc.scalar)[j % 2].dma_start(out[:, cols], result[:, cols])
